import numpy as np
import ml_dtypes


def mxq(x, axis, fmt="e4m3"):
    dtype, down = {"e4m3": (ml_dtypes.float8_e4m3fn, 7), "e5m2": (ml_dtypes.float8_e5m2, 14)}[fmt]
    v = np.moveaxis(np.asarray(x, np.float32).astype(ml_dtypes.bfloat16).astype(np.float64), axis, -1)
    blocks = v.reshape(v.shape[:-1] + (-1, 32))
    amax = np.abs(blocks).max(-1, keepdims=True)
    byte = np.maximum(np.where(amax > 0, np.frexp(amax)[1] - 1 + 127, 0) - down, 1)
    scale = np.exp2(byte - 127.0)
    codes = (blocks / scale).astype(np.float32).astype(dtype).astype(np.float64)
    return np.moveaxis((codes * scale).reshape(v.shape), -1, axis)


WIDE = False


def mx_kscale(k):
    if not WIDE:
        return np.ones(k)
    levels = np.array([10, -10, 5, -5, 0])
    if k % 512:
        return np.exp2(np.random.permutation(np.resize(levels, k // 32))).repeat(32)
    a = np.empty((k // 512, 16))
    for p in range(k // 512):
        a[p, :8] = np.random.permutation(np.resize(levels, 8))
        for g in range(8):
            far = levels[np.abs(levels - a[p, g]) >= 10]
            a[p, g + 8] = far[np.random.randint(len(far))]
    return np.exp2(a.ravel()).repeat(32)


def f64(x):
    return np.asarray(x).astype(np.float64)


def striped8(idx):
    return np.asarray(idx).reshape(8, -1, 16).transpose(0, 2, 1).reshape(128, -1).astype(np.uint16)


def unstriped8(offs):
    return offs.reshape(8, 16, -1).transpose(0, 2, 1).reshape(8, -1).astype(np.int64)


def pick8(x, idx, run):
    r = np.arange(len(x))
    return x[r[:, None], idx[r % (8 * run) // run]]


E2M1 = np.array([0.0, 0.5, 1.0, 1.5, 2.0, 3.0, 4.0, 6.0, -0.0, -0.5, -1.0, -1.5, -2.0, -3.0, -4.0, -6.0])


def pack_weight(w, fmt):
    k, n = w.shape
    w = f64(np.asarray(w, np.float32).astype(ml_dtypes.bfloat16)).reshape(k // 32, 32, n)
    amax = np.abs(w).max(1)
    if fmt == "e4m3":
        byte = np.frexp(amax)[1] - 1 + 127 - 7
    else:
        mant, ex = np.frexp(amax / 6.0)
        byte = np.where(mant > 0.5, ex, ex - 1) + 127
    byte = np.clip(np.where(amax > 0, byte, 1), 1, 254)
    scaled = (w * np.exp2(127.0 - byte)[:, None, :]).reshape(k, n).astype(np.float32)
    by_word = np.ascontiguousarray(scaled.reshape(k // 512, 128, 4, n).transpose(0, 1, 3, 2))
    if fmt == "e4m3":
        words = by_word.astype(ml_dtypes.float8_e4m3fn).view(np.uint8)
    else:
        c = by_word.astype(ml_dtypes.float4_e2m1fn).view(np.uint8) & 0xF
        words = (c[..., 0::2] | (c[..., 1::2] << 4)).reshape(k // 512, 128, 2 * n)
    return np.ascontiguousarray(words), np.ascontiguousarray(byte.astype(np.uint8).reshape(k // 512, 16, n))


def unpack_weight(words, scales, fmt):
    g, _, n = scales.shape
    words = np.ascontiguousarray(words).reshape(g, 128, n, -1)
    if fmt == "e4m3":
        vals = words.view(ml_dtypes.float8_e4m3fn).astype(np.float64)
    else:
        nib = np.empty((g, 128, n, 4), np.uint8)
        nib[..., 0::2] = words & 0xF
        nib[..., 1::2] = words >> 4
        vals = E2M1[nib]
    vals = vals * np.repeat(np.exp2(scales.astype(np.float64) - 127.0), 8, axis=1)[..., None]
    return vals.transpose(0, 1, 3, 2).reshape(g * 512, n)


D, T, U, I, J, Q = 512, 1024, 1024, 512, 256, 128


def setup_inputs():
    n = np.random.standard_normal
    idx = np.stack([np.random.permutation(T)[:J] for _ in range(8)])
    idx2 = np.stack([np.random.permutation(U)[:J] for _ in range(8)])
    idx3 = np.stack([np.random.permutation(U)[:J] for _ in range(8)])
    idx4 = np.stack([np.random.permutation(T)[:J] for _ in range(8)])
    idx5 = np.stack([np.random.permutation(T)[:I] for _ in range(8)])
    idx6 = np.stack([np.random.permutation(T)[:I] for _ in range(8)])
    fd = mx_kscale(D)
    keysp = pack_weight(n((D, T)) / fd[:, None], "e4m3")
    notesp = pack_weight(n((D, U)) / fd[:, None], "e2m1")
    return {
        "query": (n((D, Q)) * 1.0 / np.sqrt(D) * fd[:, None]).astype(np.float32),
        "keys_words": keysp[0],
        "keys_scales": keysp[1],
        "notes_words": notesp[0],
        "notes_scales": notesp[1],
        "offs": striped8(idx),
        "offs2": striped8(idx2),
        "offs3": striped8(idx3),
        "offs4": striped8(idx4),
        "offs5": striped8(idx5),
        "offs6": striped8(idx6),
    }


def reference(query, keys_words, keys_scales, notes_words, notes_scales, offs, offs2, offs3, offs4, offs5, offs6):
    idx = unstriped8(offs)
    idx2 = unstriped8(offs2)
    idx3 = unstriped8(offs3)
    idx4 = unstriped8(offs4)
    idx5 = unstriped8(offs5)
    idx6 = unstriped8(offs6)
    keysu = unpack_weight(keys_words, keys_scales, "e4m3")
    notesu = unpack_weight(notes_words, notes_scales, "e2m1")
    queryq = mxq(f64(query), 0, "e4m3")
    a = queryq.T @ keysu
    b = queryq.T @ notesu
    w = np.concatenate([pick8(a, idx, 16), pick8(b, idx2, 16)], axis=1)
    v = np.concatenate([pick8(b, idx3, 16), pick8(a, idx4, 16)], axis=1)
    r = np.maximum(w, v)
    f1 = np.zeros((Q, T))
    f1[np.arange(Q)[:, None], idx5[np.arange(Q) % 128 // 16]] = r
    aa = a - f1
    y = pick8(aa, idx6, 16) + v
    return y

@@ -1,0 +1,126 @@
+from contextlib import ExitStack
+
+import concourse.mybir as mybir
+
+D, T, U, I, J, Q = 512, 1024, 1024, 512, 256, 128
+FLOPS = 2 * D * Q * (T + U)
+
+F32 = mybir.dt.float32
+BF16 = mybir.dt.bfloat16
+I32 = mybir.dt.int32
+U32 = mybir.dt.uint32
+U16 = mybir.dt.uint16
+U8 = mybir.dt.uint8
+FP8X4 = mybir.dt.float8_e4m3fn_x4
+FP4X4 = mybir.dt.float4_e2m1fn_x4
+ALU = mybir.AluOpType
+COPY = mybir.ActivationFunctionType.Copy
+
+P = 128
+PACK = 4
+NB = 256
+
+
+def tile_attend_halfswap_two_kernel(
+    tc, query, keys_words, keys_scales, notes_words, notes_scales, offs, offs2, offs3, offs4, offs5, offs6, out
+):
+    nc = tc.nc
+    with ExitStack() as ctx:
+        lists = ctx.enter_context(tc.tile_pool(name="lists", bufs=1))
+        sb = ctx.enter_context(tc.tile_pool(name="sb", bufs=1))
+        psum = ctx.enter_context(tc.psum_pool(name="psum", bufs=1))
+
+        n_plane = sb.tile([P, U], U8, align_bytes=64)
+        k_plane = sb.tile([P, T], U8, align_bytes=64)
+        f1 = sb.tile([P, T], F32)
+        nc.vector.memset(n_plane[:].bitcast(I32), 0)
+        nc.vector.memset(k_plane[:].bitcast(I32), 0)
+        nc.vector.memset(f1[:], 0.0)
+
+        def load_plane(plane, scales):
+            for quad in range(4):
+                nc.sync.dma_start(
+                    out=plane[32 * quad : 32 * quad + 4, :].bitcast(I32),
+                    in_=scales[0, 4 * quad : 4 * quad + 4, :].bitcast(I32),
+                )
+
+        def load_list(src, name):
+            tile = lists.tile(list(src.shape), U16, name=name)
+            nc.sync.dma_start(tile[:], src)
+            return tile
+
+        q_raw = sb.tile([P, PACK, Q], F32)
+        nc.sync.dma_start(out=q_raw[:], in_=query.rearrange("(p j) q -> p j q", j=PACK))
+        load_plane(n_plane, notes_scales)
+        n_words = sb.tile([P, 2 * U], U8, align_bytes=64)
+        nc.sync.dma_start(out=n_words[:].bitcast(I32), in_=notes_words[0].bitcast(I32))
+        k_words = sb.tile([P, T], U32, align_bytes=64)
+        nc.sync.dma_start(
+            out=k_words[:].bitcast(I32), in_=keys_words[0].rearrange("p t r -> p (t r)").bitcast(I32)
+        )
+        load_plane(k_plane, keys_scales)
+        l3 = load_list(offs3, "l3")
+        l2 = load_list(offs2, "l2")
+        l1 = load_list(offs, "l1")
+        l4 = load_list(offs4, "l4")
+        l5 = load_list(offs5, "l5")
+        l6 = load_list(offs6, "l6")
+
+        q_grouped = sb.tile([P, Q, PACK], BF16, align_bytes=64)
+        nc.vector.tensor_copy(out=q_grouped[:], in_=q_raw[:].rearrange("p j q -> p q j"))
+        q_codes = sb.tile([P, Q], U32, align_bytes=64)
+        q_plane = sb.tile([P, Q], U8, align_bytes=64)
+        nc.vector.quantize_mx(
+            out=q_codes[:].bitcast(FP8X4), scales=q_plane[:], in_=q_grouped[:].rearrange("p q j -> p (q j)")
+        )
+
+        a = sb.tile([P, T], F32)
+        b = sb.tile([P, U], F32)
+        w = sb.tile([P, I], F32)
+        v = sb.tile([P, I], F32)
+
+        def score(name, rhs, plane, cols):
+            bank = psum.tile([P, NB], F32, name=name)
+            nc.tensor.matmul_mx(
+                out=bank[:],
+                lhsT=q_codes[:].bitcast(FP8X4),
+                lhsT_scale=q_plane[:],
+                rhs=rhs,
+                rhs_scale=plane[:, cols],
+                start=True,
+                stop=True,
+            )
+            return bank
+
+        for c in range(U // NB):
+            cols = slice(c * NB, (c + 1) * NB)
+            rhs = n_words[:, 2 * c * NB : 2 * (c + 1) * NB].bitcast(FP4X4)
+            bank = score("b%d" % c, rhs, n_plane, cols)
+            if c % 2 == 0:
+                nc.scalar.copy(out=b[:, cols], in_=bank[:])
+            else:
+                nc.vector.tensor_copy(out=b[:, cols], in_=bank[:])
+        nc.vector.tensor_copy(v[:, :J], b[:].indirect(l3[:]))
+        nc.vector.tensor_copy(w[:, J:], b[:].indirect(l2[:]))
+        for c in range(T // NB):
+            cols = slice(c * NB, (c + 1) * NB)
+            bank = score("a%d" % c, k_words[:, cols].bitcast(FP8X4), k_plane, cols)
+            nc.scalar.copy(out=a[:, cols], in_=bank[:])
+        nc.vector.tensor_copy(w[:, :J], a[:].indirect(l1[:]))
+        nc.scalar.activation(v[:, J:], a[:].indirect(l4[:]), COPY)
+
+        r = sb.tile([P, I], F32)
+        nc.vector.tensor_tensor(r[:], w[:], v[:], ALU.max)
+        nc.vector.tensor_copy(f1[:].indirect(l5[:]), r[:])
+        aa = sb.tile([P, T], F32)
+        nc.vector.tensor_tensor(aa[:], a[:], f1[:], ALU.subtract)
+
+        half = J // 16
+        y0 = sb.tile([P, J], F32)
+        g1 = sb.tile([P, J], F32)
+        y1 = sb.tile([P, J], F32)
+        nc.vector.tensor_tensor(y0[:], aa[:].indirect(l6[:, :half]), v[:, :J], ALU.add)
+        nc.scalar.activation(g1[:], aa[:].indirect(l6[:, half:]), COPY)
+        nc.sync.dma_start(out=out[:, :J], in_=y0[:])
+        nc.vector.tensor_tensor(y1[:], g1[:], v[:, J:], ALU.add)
+        nc.sync.dma_start(out=out[:, J:], in_=y1[:])

@@ -37,8 +37,8 @@ def tile_attend_halfswap_two_kernel(
         nc.vector.memset(k_plane[:].bitcast(I32), 0)
         nc.vector.memset(f1[:], 0.0)
 
-        def load_plane(plane, scales):
-            for quad in range(4):
+        def load_plane(plane, scales, quads):
+            for quad in quads:
                 nc.sync.dma_start(
                     out=plane[32 * quad : 32 * quad + 4, :].bitcast(I32),
                     in_=scales[0, 4 * quad : 4 * quad + 4, :].bitcast(I32),
@@ -51,14 +51,16 @@ def tile_attend_halfswap_two_kernel(
 
         q_raw = sb.tile([P, PACK, Q], F32)
         nc.sync.dma_start(out=q_raw[:], in_=query.rearrange("(p j) q -> p j q", j=PACK))
-        load_plane(n_plane, notes_scales)
+        load_plane(n_plane, notes_scales, (0, 1))
         n_words = sb.tile([P, 2 * U], U8, align_bytes=64)
         nc.sync.dma_start(out=n_words[:].bitcast(I32), in_=notes_words[0].bitcast(I32))
+        load_plane(n_plane, notes_scales, (2, 3))
+        load_plane(k_plane, keys_scales, (0,))
         k_words = sb.tile([P, T], U32, align_bytes=64)
         nc.sync.dma_start(
             out=k_words[:].bitcast(I32), in_=keys_words[0].rearrange("p t r -> p (t r)").bitcast(I32)
         )
-        load_plane(k_plane, keys_scales)
+        load_plane(k_plane, keys_scales, (1, 2, 3))
         l3 = load_list(offs3, "l3")
         l2 = load_list(offs2, "l2")
         l1 = load_list(offs, "l1")
@@ -67,7 +69,10 @@ def tile_attend_halfswap_two_kernel(
         l6 = load_list(offs6, "l6")
 
         q_grouped = sb.tile([P, Q, PACK], BF16, align_bytes=64)
-        nc.vector.tensor_copy(out=q_grouped[:], in_=q_raw[:].rearrange("p j q -> p q j"))
+        dst = q_grouped[:].rearrange("p (c i) j -> p c j i", i=4)
+        src = q_raw[:].rearrange("p j (c i) -> p c j i", i=4)
+        nc.vector.tensor_copy(out=dst[:, :20], in_=src[:, :20])
+        nc.scalar.copy(out=dst[:, 20:], in_=src[:, 20:])
         q_codes = sb.tile([P, Q], U32, align_bytes=64)
         q_plane = sb.tile([P, Q], U8, align_bytes=64)
         nc.vector.quantize_mx(

@@ -33,8 +33,6 @@ def tile_attend_halfswap_two_kernel(
         n_plane = sb.tile([P, U], U8, align_bytes=64)
         k_plane = sb.tile([P, T], U8, align_bytes=64)
         f1 = sb.tile([P, T], F32)
-        nc.vector.memset(n_plane[:].bitcast(I32), 0)
-        nc.vector.memset(k_plane[:].bitcast(I32), 0)
         nc.vector.memset(f1[:], 0.0)
 
         def load_plane(plane, scales, quads):
@@ -107,18 +105,25 @@ def tile_attend_halfswap_two_kernel(
                 nc.vector.tensor_copy(out=b[:, cols], in_=bank[:])
         nc.vector.tensor_copy(v[:, :J], b[:].indirect(l3[:]))
         nc.vector.tensor_copy(w[:, J:], b[:].indirect(l2[:]))
+        a_banks = []
         for c in range(T // NB):
             cols = slice(c * NB, (c + 1) * NB)
             bank = score("a%d" % c, k_words[:, cols].bitcast(FP8X4), k_plane, cols)
             nc.scalar.copy(out=a[:, cols], in_=bank[:])
+            a_banks.append(bank)
         nc.vector.tensor_copy(w[:, :J], a[:].indirect(l1[:]))
         nc.scalar.activation(v[:, J:], a[:].indirect(l4[:]), COPY)
 
         r = sb.tile([P, I], F32)
-        nc.vector.tensor_tensor(r[:], w[:], v[:], ALU.max)
+        nc.vector.tensor_tensor(r[:, :J], w[:, :J], v[:, :J], ALU.max)
+        nc.vector.tensor_tensor(r[:, J:], w[:, J:], v[:, J:], ALU.max)
         nc.vector.tensor_copy(f1[:].indirect(l5[:]), r[:])
         aa = sb.tile([P, T], F32)
-        nc.vector.tensor_tensor(aa[:], a[:], f1[:], ALU.subtract)
+        last = slice(T - NB, T)
+        nc.gpsimd.tensor_tensor(aa[:, last], a[:, last], f1[:, last], ALU.subtract)
+        for c in range(T // NB - 1):
+            cols = slice(c * NB, (c + 1) * NB)
+            nc.vector.tensor_tensor(aa[:, cols], a_banks[c][:], f1[:, cols], ALU.subtract)
 
         half = J // 16
         y0 = sb.tile([P, J], F32)

from contextlib import ExitStack

import concourse.mybir as mybir

D, T, U, I, J, Q = 512, 1024, 1024, 512, 256, 128
FLOPS = 2 * D * Q * (T + U)

F32 = mybir.dt.float32
BF16 = mybir.dt.bfloat16
I32 = mybir.dt.int32
U32 = mybir.dt.uint32
U16 = mybir.dt.uint16
U8 = mybir.dt.uint8
FP8X4 = mybir.dt.float8_e4m3fn_x4
FP4X4 = mybir.dt.float4_e2m1fn_x4
ALU = mybir.AluOpType
COPY = mybir.ActivationFunctionType.Copy

P = 128
PACK = 4
NB = 256


def tile_attend_halfswap_two_kernel(
    tc, query, keys_words, keys_scales, notes_words, notes_scales, offs, offs2, offs3, offs4, offs5, offs6, out
):
    nc = tc.nc
    with ExitStack() as ctx:
        lists = ctx.enter_context(tc.tile_pool(name="lists", bufs=1))
        sb = ctx.enter_context(tc.tile_pool(name="sb", bufs=1))
        psum = ctx.enter_context(tc.psum_pool(name="psum", bufs=1))

        n_plane = sb.tile([P, U], U8, align_bytes=64)
        k_plane = sb.tile([P, T], U8, align_bytes=64)
        f1 = sb.tile([P, T], F32)
        nc.vector.memset(f1[:], 0.0)

        def load_plane(plane, scales, quads):
            for quad in quads:
                nc.sync.dma_start(
                    out=plane[32 * quad : 32 * quad + 4, :].bitcast(I32),
                    in_=scales[0, 4 * quad : 4 * quad + 4, :].bitcast(I32),
                )

        def load_list(src, name):
            tile = lists.tile(list(src.shape), U16, name=name)
            nc.sync.dma_start(tile[:], src)
            return tile

        q_raw = sb.tile([P, PACK, Q], F32)
        nc.sync.dma_start(out=q_raw[:], in_=query.rearrange("(p j) q -> p j q", j=PACK))
        load_plane(n_plane, notes_scales, (0, 1))
        n_words = sb.tile([P, 2 * U], U8, align_bytes=64)
        nc.sync.dma_start(out=n_words[:].bitcast(I32), in_=notes_words[0].bitcast(I32))
        load_plane(n_plane, notes_scales, (2, 3))
        load_plane(k_plane, keys_scales, (0,))
        k_words = sb.tile([P, T], U32, align_bytes=64)
        nc.sync.dma_start(
            out=k_words[:].bitcast(I32), in_=keys_words[0].rearrange("p t r -> p (t r)").bitcast(I32)
        )
        load_plane(k_plane, keys_scales, (1, 2, 3))
        l3 = load_list(offs3, "l3")
        l2 = load_list(offs2, "l2")
        l1 = load_list(offs, "l1")
        l4 = load_list(offs4, "l4")
        l5 = load_list(offs5, "l5")
        l6 = load_list(offs6, "l6")

        q_grouped = sb.tile([P, Q, PACK], BF16, align_bytes=64)
        dst = q_grouped[:].rearrange("p (c i) j -> p c j i", i=4)
        src = q_raw[:].rearrange("p j (c i) -> p c j i", i=4)
        nc.vector.tensor_copy(out=dst[:, :20], in_=src[:, :20])
        nc.scalar.copy(out=dst[:, 20:], in_=src[:, 20:])
        q_codes = sb.tile([P, Q], U32, align_bytes=64)
        q_plane = sb.tile([P, Q], U8, align_bytes=64)
        nc.vector.quantize_mx(
            out=q_codes[:].bitcast(FP8X4), scales=q_plane[:], in_=q_grouped[:].rearrange("p q j -> p (q j)")
        )

        a = sb.tile([P, T], F32)
        b = sb.tile([P, U], F32)
        w = sb.tile([P, I], F32)
        v = sb.tile([P, I], F32)

        def score(name, rhs, plane, cols):
            bank = psum.tile([P, NB], F32, name=name)
            nc.tensor.matmul_mx(
                out=bank[:],
                lhsT=q_codes[:].bitcast(FP8X4),
                lhsT_scale=q_plane[:],
                rhs=rhs,
                rhs_scale=plane[:, cols],
                start=True,
                stop=True,
            )
            return bank

        for c in range(U // NB):
            cols = slice(c * NB, (c + 1) * NB)
            rhs = n_words[:, 2 * c * NB : 2 * (c + 1) * NB].bitcast(FP4X4)
            bank = score("b%d" % c, rhs, n_plane, cols)
            if c % 2 == 0:
                nc.scalar.copy(out=b[:, cols], in_=bank[:])
            else:
                nc.vector.tensor_copy(out=b[:, cols], in_=bank[:])
        nc.vector.tensor_copy(v[:, :J], b[:].indirect(l3[:]))
        nc.vector.tensor_copy(w[:, J:], b[:].indirect(l2[:]))
        a_banks = []
        for c in range(T // NB):
            cols = slice(c * NB, (c + 1) * NB)
            bank = score("a%d" % c, k_words[:, cols].bitcast(FP8X4), k_plane, cols)
            nc.scalar.copy(out=a[:, cols], in_=bank[:])
            a_banks.append(bank)
        nc.vector.tensor_copy(w[:, :J], a[:].indirect(l1[:]))
        nc.scalar.activation(v[:, J:], a[:].indirect(l4[:]), COPY)

        r = sb.tile([P, I], F32)
        nc.vector.tensor_tensor(r[:, :J], w[:, :J], v[:, :J], ALU.max)
        nc.vector.tensor_tensor(r[:, J:], w[:, J:], v[:, J:], ALU.max)
        nc.vector.tensor_copy(f1[:].indirect(l5[:]), r[:])
        aa = sb.tile([P, T], F32)
        last = slice(T - NB, T)
        nc.gpsimd.tensor_tensor(aa[:, last], a[:, last], f1[:, last], ALU.subtract)
        for c in range(T // NB - 1):
            cols = slice(c * NB, (c + 1) * NB)
            nc.vector.tensor_tensor(aa[:, cols], a_banks[c][:], f1[:, cols], ALU.subtract)

        half = J // 16
        y0 = sb.tile([P, J], F32)
        g1 = sb.tile([P, J], F32)
        y1 = sb.tile([P, J], F32)
        nc.vector.tensor_tensor(y0[:], aa[:].indirect(l6[:, :half]), v[:, :J], ALU.add)
        nc.scalar.activation(g1[:], aa[:].indirect(l6[:, half:]), COPY)
        nc.sync.dma_start(out=out[:, :J], in_=y0[:])
        nc.vector.tensor_tensor(y1[:], g1[:], v[:, J:], ALU.add)
        nc.sync.dma_start(out=out[:, J:], in_=y1[:])
